import numpy as np
import ml_dtypes


def mxq(x, axis, fmt="e4m3"):
    dtype, down = {"e4m3": (ml_dtypes.float8_e4m3fn, 7), "e5m2": (ml_dtypes.float8_e5m2, 14)}[fmt]
    v = np.moveaxis(np.asarray(x, np.float32).astype(ml_dtypes.bfloat16).astype(np.float64), axis, -1)
    blocks = v.reshape(v.shape[:-1] + (-1, 32))
    amax = np.abs(blocks).max(-1, keepdims=True)
    byte = np.maximum(np.where(amax > 0, np.frexp(amax)[1] - 1 + 127, 0) - down, 1)
    scale = np.exp2(byte - 127.0)
    codes = (blocks / scale).astype(np.float32).astype(dtype).astype(np.float64)
    return np.moveaxis((codes * scale).reshape(v.shape), -1, axis)


WIDE = False


def mx_kscale(k):
    if not WIDE:
        return np.ones(k)
    levels = np.array([10, -10, 5, -5, 0])
    if k % 512:
        return np.exp2(np.random.permutation(np.resize(levels, k // 32))).repeat(32)
    a = np.empty((k // 512, 16))
    for p in range(k // 512):
        a[p, :8] = np.random.permutation(np.resize(levels, 8))
        for g in range(8):
            far = levels[np.abs(levels - a[p, g]) >= 10]
            a[p, g + 8] = far[np.random.randint(len(far))]
    return np.exp2(a.ravel()).repeat(32)


def f64(x):
    return np.asarray(x).astype(np.float64)


def striped(idx):
    return np.tile(idx.reshape(-1, 16).T, (8, 1)).astype(np.uint16)


def unstriped(offs):
    return offs[:16].T.reshape(-1).astype(np.int64)


def silu(v):
    return v / (1.0 + np.exp(-np.maximum(v, -700.0)))


K, T, S, D, H, N = 1024, 1024, 512, 2, 512, 128


def setup_inputs():
    n = np.random.standard_normal
    s = mx_kscale(K)[:, None]
    u = mx_kscale(H)
    return {
        "xT": (n((K, T)) * s).astype(np.float32),
        "w1": (n((K, H)) / np.sqrt(K) / s * u).astype(np.float32),
        "w2": (n((H, N)) / np.sqrt(H) / u[:, None]).astype(np.float32),
        "taps": (n((H, D)) / np.sqrt(D)).astype(np.float32),
        "offs": striped(np.random.permutation(T)[:S]),
    }


def reference(xT, w1, w2, taps, offs):
    xq = mxq(f64(xT)[:, unstriped(offs)], 0, "e4m3")
    h = mxq(f64(w1), 0, "e4m3").T @ xq
    z = silu(f64(taps)[:, 0:1] * h + f64(taps)[:, 1:2] * (np.pad(h, ((0, 0), (1, 0)))[:, :S]))
    return mxq(f64(w2), 0, "e4m3").T @ mxq(z, 0, "e4m3")

@@ -1,0 +1,234 @@
+from contextlib import ExitStack
+
+import concourse.mybir as mybir
+
+K, T, S, H, N = 1024, 1024, 512, 512, 128
+FLOPS = 2 * K * H * S + 2 * H * N * S
+
+F32 = mybir.dt.float32
+BF16 = mybir.dt.bfloat16
+U32 = mybir.dt.uint32
+U16 = mybir.dt.uint16
+U8 = mybir.dt.uint8
+FP8X4 = mybir.dt.float8_e4m3fn_x4
+ACT = mybir.ActivationFunctionType
+ALU = mybir.AluOpType
+
+P = 128
+PACK = 4
+K_PASS = P * PACK
+HALF = S // 2
+LEAD = 4
+SCALAR_COLS = 50
+
+
+def tile_picked_dconv_silu_e_kernel(tc, xT, w1, w2, taps, offs, out):
+    nc = tc.nc
+
+    with ExitStack() as ctx:
+        keep = ctx.enter_context(tc.tile_pool(name="keep", bufs=1))
+        psum = ctx.enter_context(tc.psum_pool(name="psum", bufs=1))
+
+        def sbuf(shape, dtype, name):
+            return keep.tile(shape, dtype, name=name, align_bytes=64)
+
+        offsets = keep.tile([P, S // 16], U16, name="offsets")
+        nc.sync.dma_start(offsets[:], offs)
+        tap = sbuf([P, PACK * 2], F32, "tap")
+        nc.sync.dma_start(tap[:], taps.rearrange("(p t) d -> p (t d)", t=PACK))
+
+        x_rows = xT.rearrange("(g p j) w -> g j p w", p=P, j=PACK)
+        w1_rows = w1.rearrange("(g p j) c -> g p (j c)", p=P, j=PACK)
+        x_raw, w1_raw = {}, {}
+        for g in range(2):
+            for j in range(PACK):
+                x_raw[g, j] = sbuf([P, T], F32, f"x_raw{g}{j}")
+                nc.sync.dma_start(x_raw[g, j][:], x_rows[g, j])
+            w1_raw[g] = sbuf([P, PACK * H], F32, f"w1_raw{g}")
+            nc.sync.dma_start(w1_raw[g][:], w1_rows[g])
+        w2_raw = sbuf([P, PACK * N], F32, "w2_raw")
+        nc.sync.dma_start(w2_raw[:], w2.rearrange("(p j) n -> p (j n)", j=PACK))
+
+        delayed = sbuf([P, PACK, LEAD + S], F32, "delayed")
+        zeros = sbuf([P, PACK], F32, "zeros")
+        nc.gpsimd.memset(zeros[:], 0.0)
+        nc.scalar.activation(delayed[:, :, LEAD - 1], zeros[:], ACT.Silu)
+
+        def quantize(grouped_ap, codes, scales):
+            nc.vector.quantize_mx(out=codes.bitcast(FP8X4), scales=scales, in_=grouped_ap)
+
+        def shared(shape, dtype, name, tag):
+            return keep.tile(shape, dtype, name=name, tag=tag, align_bytes=64)
+
+        w1_grouped = [sbuf([P, PACK, P, PACK], BF16, f"w1_grouped{g}") for g in range(2)]
+        w1_codes = [sbuf([P, H], U32, f"w1_codes{g}") for g in range(2)]
+        w1_scales = [sbuf([P, H], U8, f"w1_scales{g}") for g in range(2)]
+        x_codes, x_scales = {}, {}
+
+        def gather(dst, g, j):
+            nc.vector.tensor_copy(out=dst, in_=x_raw[g, j][:].indirect(offsets[:]))
+
+        def gather_on_scalar(dst, g, j):
+            rounded = sbuf([P, T], BF16, f"rounded{g}")
+            nc.scalar.activation(rounded[:], x_raw[g, j][:], ACT.Copy)
+            nc.scalar.activation(dst, rounded[:].indirect(offsets[:]), ACT.Copy)
+
+        def cast_w1(copy, g, m0, m1):
+            copy(
+                out=w1_grouped[g][:].rearrange("p t m j -> p m j t")[:, m0:m1],
+                in_=w1_raw[g][:].rearrange("p (j m t) -> p m j t", j=PACK, t=PACK)[:, m0:m1],
+            )
+
+        def quantize_w1(g, t0, t1):
+            cols = slice(t0 * P, t1 * P)
+            quantize(w1_grouped[g][:, t0:t1].rearrange("p t m j -> p (t m j)"), w1_codes[g][:, cols], w1_scales[g][:, cols])
+
+        picked_first = sbuf([P, PACK, S], BF16, "picked_first")
+        gather(picked_first[:, 0, :], 0, 0)
+        gather_on_scalar(picked_first[:, 1, :], 0, 1)
+        gather(picked_first[:, 2, :], 0, 2)
+        gather(picked_first[:, 3, :], 0, 3)
+        x_grouped_first = sbuf([P, S, PACK], BF16, "x_grouped_first")
+        nc.vector.tensor_copy(
+            out=x_grouped_first[:].rearrange("p (c i) j -> p c j i", i=4),
+            in_=picked_first[:].rearrange("p j (c i) -> p c j i", i=4),
+        )
+        codes_first = sbuf([P, S], U32, "codes_first")
+        scales_first = sbuf([P, S], U8, "scales_first")
+        quantize(x_grouped_first[:].rearrange("p n j -> p (n j)"), codes_first[:], scales_first[:])
+        for h in range(2):
+            x_codes[0, h] = codes_first[:, h * HALF : (h + 1) * HALF]
+            x_scales[0, h] = scales_first[:, h * HALF : (h + 1) * HALF]
+        cast_w1(nc.scalar.copy, 0, 0, P)
+
+        picked = [sbuf([P, 2, S], BF16, f"picked{u}") for u in range(2)]
+        x_grouped = [sbuf([P, HALF, PACK], BF16, f"x_grouped{h}") for h in range(2)]
+
+        def weave(copy, u, h):
+            copy(
+                out=x_grouped[h][:, :, 2 * u : 2 * u + 2],
+                in_=picked[u][:, :, h * HALF : (h + 1) * HALF].rearrange("p e n -> p n e"),
+            )
+
+        def quantize_x(h, scale_tag):
+            codes = sbuf([P, HALF], U32, f"x_codes{h}")
+            scales = shared([P, HALF], U8, f"x_scales{h}", scale_tag)
+            quantize(x_grouped[h][:].rearrange("p n j -> p (n j)"), codes[:], scales[:])
+            x_codes[1, h], x_scales[1, h] = codes[:], scales[:]
+
+        gather(picked[0][:, 0, :], 1, 0)
+        quantize_w1(0, 0, PACK)
+        gather_on_scalar(picked[0][:, 1, :], 1, 1)
+        for h in range(2):
+            weave(nc.scalar.copy, 0, h)
+        gather(picked[1][:, 0, :], 1, 2)
+        gather(picked[1][:, 1, :], 1, 3)
+        weave(nc.vector.tensor_copy, 1, 0)
+        weave(nc.scalar.copy, 1, 1)
+        quantize_x(0, "x_scales0")
+
+        banks = {}
+        for h in range(2):
+            for t in range(PACK):
+                banks[t, h] = psum.tile([P, HALF], F32, name=f"h{t}{h}", tag=f"bank{t}{h}")
+
+        def first_product(g, t, h):
+            m_cols = slice(t * P, (t + 1) * P)
+            nc.tensor.matmul_mx(
+                out=banks[t, h][:],
+                lhsT=w1_codes[g][:, m_cols].bitcast(FP8X4),
+                lhsT_scale=w1_scales[g][:, m_cols],
+                rhs=x_codes[g, h].bitcast(FP8X4),
+                rhs_scale=x_scales[g, h],
+                start=(g == 0),
+                stop=(g == 1),
+            )
+
+        for h in range(2):
+            for t in range(PACK):
+                first_product(0, t, h)
+
+        cast_w1(nc.scalar.copy, 1, 0, SCALAR_COLS)
+        cast_w1(nc.vector.tensor_copy, 1, SCALAR_COLS, P)
+        for t in range(PACK):
+            quantize_w1(1, t, t + 1)
+        quantize_x(1, "w1_grouped1")
+        for h in range(2):
+            for t in range(PACK):
+                first_product(1, t, h)
+
+        w2_grouped = shared([P, N, PACK], BF16, "w2_grouped", "x_grouped1")
+        w2_codes = sbuf([P, N], U32, "w2_codes")
+        w2_scales = sbuf([P, N], U8, "w2_scales")
+
+        conv = {
+            (h, c0): sbuf([P, PACK, width], F32, f"conv{h}{c0}")
+            for h, c0, width in ((0, 0, HALF), (1, 0, HALF // 2), (1, HALF // 2, HALF // 2))
+        }
+
+        def delay(t, h, on_vector):
+            dst = delayed[:, t, LEAD + h * HALF : LEAD + (h + 1) * HALF]
+            if on_vector:
+                nc.vector.tensor_scalar(dst, banks[t, h][:], tap[:, 2 * t + 1 : 2 * t + 2], None, ALU.mult)
+            else:
+                nc.scalar.activation(dst, banks[t, h][:], ACT.Copy, scale=tap[:, 2 * t + 1 : 2 * t + 2])
+
+        def convolve(t, h, c0=0, c1=HALF):
+            nc.vector.scalar_tensor_tensor(
+                out=conv[h, c0][:, t, :],
+                in0=banks[t, h][:, c0:c1],
+                scalar=tap[:, 2 * t : 2 * t + 1],
+                in1=delayed[:, t, LEAD - 1 + h * HALF + c0 : LEAD - 1 + h * HALF + c1],
+                op0=ALU.mult,
+                op1=ALU.add,
+            )
+
+        def activate(h, c0, c1):
+            z = sbuf([P, c1 - c0, PACK], BF16, f"z{h}{c0}")
+            nc.scalar.activation(
+                z[:].rearrange("p (c i) t -> p c t i", i=4),
+                conv[h, c0][:].rearrange("p t (c i) -> p c t i", i=4),
+                ACT.Silu,
+            )
+            return z
+
+        def second_product(z, n0, width, tag, copy):
+            z_codes = sbuf([P, width], U32, f"z_codes{n0}")
+            z_scales = sbuf([P, width], U8, f"z_scales{n0}")
+            quantize(z[:].rearrange("p n t -> p (n t)"), z_codes[:], z_scales[:])
+            acc = psum.tile([P, width], F32, name=f"acc{n0}", tag=tag)
+            nc.tensor.matmul_mx(
+                out=acc[:],
+                lhsT=w2_codes[:].bitcast(FP8X4),
+                lhsT_scale=w2_scales[:],
+                rhs=z_codes[:].bitcast(FP8X4),
+                rhs_scale=z_scales[:],
+                start=True,
+                stop=True,
+            )
+            result = sbuf([P, width], F32, f"result{n0}")
+            copy(out=result[:], in_=acc[:])
+            nc.sync.dma_start(out[:, n0 : n0 + width], result[:])
+
+        for t in range(0, PACK, 2):
+            delay(t, 0, False)
+            delay(t + 1, 0, True)
+            convolve(t, 0)
+            convolve(t + 1, 0)
+        for t in range(PACK):
+            delay(t, 1, False)
+        z_first = activate(0, 0, HALF)
+        nc.gpsimd.tensor_copy(
+            out=w2_grouped[:].rearrange("p n j -> p n j"),
+            in_=w2_raw[:].rearrange("p (j n) -> p n j", j=PACK),
+        )
+        for t in range(PACK):
+            convolve(t, 1, 0, HALF // 2)
+        z_third = activate(1, 0, HALF // 2)
+        for t in range(PACK):
+            convolve(t, 1, HALF // 2, HALF)
+        z_fourth = activate(1, HALF // 2, HALF)
+        quantize(w2_grouped[:].rearrange("p n j -> p (n j)"), w2_codes[:], w2_scales[:])
+        second_product(z_first, 0, HALF, "bank00", nc.vector.tensor_copy)
+        second_product(z_third, HALF, HALF // 2, "bank10", nc.scalar.copy)
+        second_product(z_fourth, HALF + HALF // 2, HALF // 2, "bank20", nc.scalar.copy)

@@ -19,7 +19,8 @@ PACK = 4
 K_PASS = P * PACK
 HALF = S // 2
 LEAD = 4
-SCALAR_COLS = 50
+SCALAR_COLS = 42
+QUARTER = S // 4
 
 
 def tile_picked_dconv_silu_e_kernel(tc, xT, w1, w2, taps, offs, out):
@@ -32,20 +33,31 @@ def tile_picked_dconv_silu_e_kernel(tc, xT, w1, w2, taps, offs, out):
         def sbuf(shape, dtype, name):
             return keep.tile(shape, dtype, name=name, align_bytes=64)
 
-        offsets = keep.tile([P, S // 16], U16, name="offsets")
-        nc.sync.dma_start(offsets[:], offs)
-        tap = sbuf([P, PACK * 2], F32, "tap")
-        nc.sync.dma_start(tap[:], taps.rearrange("(p t) d -> p (t d)", t=PACK))
-
         x_rows = xT.rearrange("(g p j) w -> g j p w", p=P, j=PACK)
         w1_rows = w1.rearrange("(g p j) c -> g p (j c)", p=P, j=PACK)
         x_raw, w1_raw = {}, {}
-        for g in range(2):
-            for j in range(PACK):
-                x_raw[g, j] = sbuf([P, T], F32, f"x_raw{g}{j}")
-                nc.sync.dma_start(x_raw[g, j][:], x_rows[g, j])
+
+        def load_x(g, j):
+            x_raw[g, j] = sbuf([P, T], F32, f"x_raw{g}{j}")
+            nc.sync.dma_start(x_raw[g, j][:], x_rows[g, j])
+
+        def load_w1(g):
             w1_raw[g] = sbuf([P, PACK * H], F32, f"w1_raw{g}")
             nc.sync.dma_start(w1_raw[g][:], w1_rows[g])
+
+        load_x(0, 0)
+        offsets = keep.tile([P, S // 16], U16, name="offsets")
+        nc.sync.dma_start(offsets[:], offs)
+        for j in range(1, PACK):
+            load_x(0, j)
+        load_x(1, 0)
+        load_x(1, 1)
+        load_w1(0)
+        load_x(1, 2)
+        load_x(1, 3)
+        load_w1(1)
+        tap = sbuf([P, PACK * 2], F32, "tap")
+        nc.sync.dma_start(tap[:], taps.rearrange("(p t) d -> p (t d)", t=PACK))
         w2_raw = sbuf([P, PACK * N], F32, "w2_raw")
         nc.sync.dma_start(w2_raw[:], w2.rearrange("(p j) n -> p (j n)", j=PACK))
 
@@ -60,18 +72,24 @@ def tile_picked_dconv_silu_e_kernel(tc, xT, w1, w2, taps, offs, out):
         def shared(shape, dtype, name, tag):
             return keep.tile(shape, dtype, name=name, tag=tag, align_bytes=64)
 
-        w1_grouped = [sbuf([P, PACK, P, PACK], BF16, f"w1_grouped{g}") for g in range(2)]
+        w1_grouped = [sbuf([P, PACK, P, PACK], BF16, "w1_grouped0")]
         w1_codes = [sbuf([P, H], U32, f"w1_codes{g}") for g in range(2)]
         w1_scales = [sbuf([P, H], U8, f"w1_scales{g}") for g in range(2)]
         x_codes, x_scales = {}, {}
 
-        def gather(dst, g, j):
-            nc.vector.tensor_copy(out=dst, in_=x_raw[g, j][:].indirect(offsets[:]))
+        def entries(n0, n1):
+            return offsets[:, n0 // 16 : n1 // 16]
 
-        def gather_on_scalar(dst, g, j):
+        def gather(dst, g, j, n0=0, n1=S):
+            nc.vector.tensor_copy(out=dst, in_=x_raw[g, j][:].indirect(entries(n0, n1)))
+
+        def round_on_scalar(g, j):
             rounded = sbuf([P, T], BF16, f"rounded{g}")
             nc.scalar.activation(rounded[:], x_raw[g, j][:], ACT.Copy)
-            nc.scalar.activation(dst, rounded[:].indirect(offsets[:]), ACT.Copy)
+            return rounded
+
+        def gather_on_scalar(dst, rounded, n0=0, n1=S):
+            nc.scalar.activation(dst, rounded[:].indirect(entries(n0, n1)), ACT.Copy)
 
         def cast_w1(copy, g, m0, m1):
             copy(
@@ -85,47 +103,51 @@ def tile_picked_dconv_silu_e_kernel(tc, xT, w1, w2, taps, offs, out):
 
         picked_first = sbuf([P, PACK, S], BF16, "picked_first")
         gather(picked_first[:, 0, :], 0, 0)
-        gather_on_scalar(picked_first[:, 1, :], 0, 1)
+        gather_on_scalar(picked_first[:, 1, :], round_on_scalar(0, 1))
         gather(picked_first[:, 2, :], 0, 2)
         gather(picked_first[:, 3, :], 0, 3)
         x_grouped_first = sbuf([P, S, PACK], BF16, "x_grouped_first")
-        nc.vector.tensor_copy(
+        nc.scalar.copy(
             out=x_grouped_first[:].rearrange("p (c i) j -> p c j i", i=4),
             in_=picked_first[:].rearrange("p j (c i) -> p c j i", i=4),
         )
+        pairs = [sbuf([P, 2, HALF], BF16, f"pair{u}") for u in range(2)]
+        picked_late = sbuf([P, PACK, HALF], BF16, "picked_late")
+        x_grouped = sbuf([P, HALF, PACK], BF16, "x_grouped")
+
+        def weave_pair(copy, u):
+            copy(out=x_grouped[:, :, 2 * u : 2 * u + 2], in_=pairs[u][:].rearrange("p e n -> p n e"))
+
+        def gather_halves(j):
+            gather(pairs[j // 2][:, j % 2, :], 1, j, 0, HALF)
+            gather(picked_late[:, j, :], 1, j, HALF, S)
+
+        gather_halves(0)
+        gather_halves(1)
         codes_first = sbuf([P, S], U32, "codes_first")
         scales_first = sbuf([P, S], U8, "scales_first")
         quantize(x_grouped_first[:].rearrange("p n j -> p (n j)"), codes_first[:], scales_first[:])
         for h in range(2):
             x_codes[0, h] = codes_first[:, h * HALF : (h + 1) * HALF]
             x_scales[0, h] = scales_first[:, h * HALF : (h + 1) * HALF]
-        cast_w1(nc.scalar.copy, 0, 0, P)
-
-        picked = [sbuf([P, 2, S], BF16, f"picked{u}") for u in range(2)]
-        x_grouped = [sbuf([P, HALF, PACK], BF16, f"x_grouped{h}") for h in range(2)]
-
-        def weave(copy, u, h):
-            copy(
-                out=x_grouped[h][:, :, 2 * u : 2 * u + 2],
-                in_=picked[u][:, :, h * HALF : (h + 1) * HALF].rearrange("p e n -> p n e"),
-            )
-
-        def quantize_x(h, scale_tag):
-            codes = sbuf([P, HALF], U32, f"x_codes{h}")
-            scales = shared([P, HALF], U8, f"x_scales{h}", scale_tag)
-            quantize(x_grouped[h][:].rearrange("p n j -> p (n j)"), codes[:], scales[:])
-            x_codes[1, h], x_scales[1, h] = codes[:], scales[:]
-
-        gather(picked[0][:, 0, :], 1, 0)
+            x_codes[1, h] = sbuf([P, HALF], U32, f"x_codes{h}")[:]
+        x_scales[1, 0] = sbuf([P, HALF], U8, "x_scales0")[:]
+        weave_pair(nc.scalar.copy, 0)
+        cast_w1(nc.vector.tensor_copy, 0, SCALAR_COLS, P)
+        cast_w1(nc.scalar.copy, 0, 0, SCALAR_COLS)
         quantize_w1(0, 0, PACK)
-        gather_on_scalar(picked[0][:, 1, :], 1, 1)
-        for h in range(2):
-            weave(nc.scalar.copy, 0, h)
-        gather(picked[1][:, 0, :], 1, 2)
-        gather(picked[1][:, 1, :], 1, 3)
-        weave(nc.vector.tensor_copy, 1, 0)
-        weave(nc.scalar.copy, 1, 1)
-        quantize_x(0, "x_scales0")
+        rounded = round_on_scalar(1, 2)
+        gather_on_scalar(pairs[1][:, 0, :], rounded, 0, HALF)
+        gather_on_scalar(picked_late[:, 2, :], rounded, HALF, S)
+        gather_halves(3)
+        weave_pair(nc.vector.tensor_copy, 1)
+        quantize(x_grouped[:].rearrange("p n j -> p (n j)"), x_codes[1, 0], x_scales[1, 0])
+
+        x_grouped_late = sbuf([P, HALF, PACK], BF16, "x_grouped_late")
+        nc.scalar.copy(
+            out=x_grouped_late[:].rearrange("p (c i) j -> p c j i", i=4),
+            in_=picked_late[:].rearrange("p j (c i) -> p c j i", i=4),
+        )
 
         banks = {}
         for h in range(2):
@@ -148,23 +170,32 @@ def tile_picked_dconv_silu_e_kernel(tc, xT, w1, w2, taps, offs, out):
             for t in range(PACK):
                 first_product(0, t, h)
 
-        cast_w1(nc.scalar.copy, 1, 0, SCALAR_COLS)
-        cast_w1(nc.vector.tensor_copy, 1, SCALAR_COLS, P)
+        w1_late = [sbuf([P, 2, P, PACK], BF16, f"w1_late{u}") for u in range(2)]
+
+        def cast_w1_late(copy, u, m0, m1):
+            copy(
+                out=w1_late[u][:].rearrange("p t m j -> p m j t")[:, m0:m1],
+                in_=w1_raw[1][:].rearrange("p (j m t) -> p m j t", j=PACK, t=PACK)[:, m0:m1, :, 2 * u : 2 * u + 2],
+            )
+
+        cast_w1_late(nc.vector.tensor_copy, 0, 0, P)
+        cast_w1_late(nc.vector.tensor_copy, 1, 0, P // 2)
+        cast_w1_late(nc.scalar.copy, 1, P // 2, P)
         for t in range(PACK):
-            quantize_w1(1, t, t + 1)
-        quantize_x(1, "w1_grouped1")
+            cols = slice(t * P, (t + 1) * P)
+            quantize(w1_late[t // 2][:, t % 2].rearrange("p m j -> p (m j)"), w1_codes[1][:, cols], w1_scales[1][:, cols])
+        x_scales[1, 1] = shared([P, HALF], U8, "x_scales1", "w1_late0")[:]
+        quantize(x_grouped_late[:].rearrange("p n j -> p (n j)"), x_codes[1, 1], x_scales[1, 1])
         for h in range(2):
             for t in range(PACK):
                 first_product(1, t, h)
 
-        w2_grouped = shared([P, N, PACK], BF16, "w2_grouped", "x_grouped1")
+        w2_grouped = shared([P, N, PACK], BF16, "w2_grouped", "w1_late1")
         w2_codes = sbuf([P, N], U32, "w2_codes")
         w2_scales = sbuf([P, N], U8, "w2_scales")
 
-        conv = {
-            (h, c0): sbuf([P, PACK, width], F32, f"conv{h}{c0}")
-            for h, c0, width in ((0, 0, HALF), (1, 0, HALF // 2), (1, HALF // 2, HALF // 2))
-        }
+        conv = {(1, c0): sbuf([P, PACK, QUARTER], F32, f"conv1{c0}") for c0 in (0, QUARTER)}
+        conv[0, 0] = sbuf([P, PACK, HALF], F32, "conv00")
 
         def delay(t, h, on_vector):
             dst = delayed[:, t, LEAD + h * HALF : LEAD + (h + 1) * HALF]
@@ -210,13 +241,12 @@ def tile_picked_dconv_silu_e_kernel(tc, xT, w1, w2, taps, offs, out):
             copy(out=result[:], in_=acc[:])
             nc.sync.dma_start(out[:, n0 : n0 + width], result[:])
 
-        for t in range(0, PACK, 2):
-            delay(t, 0, False)
-            delay(t + 1, 0, True)
-            convolve(t, 0)
-            convolve(t + 1, 0)
         for t in range(PACK):
-            delay(t, 1, False)
+            delay(t, 0, t == 1)
+        for t in range(PACK):
+            convolve(t, 0)
+        for t in range(PACK):
+            delay(t, 1, t == 0)
         z_first = activate(0, 0, HALF)
         nc.gpsimd.tensor_copy(
             out=w2_grouped[:].rearrange("p n j -> p n j"),
@@ -229,6 +259,6 @@ def tile_picked_dconv_silu_e_kernel(tc, xT, w1, w2, taps, offs, out):
             convolve(t, 1, HALF // 2, HALF)
         z_fourth = activate(1, HALF // 2, HALF)
         quantize(w2_grouped[:].rearrange("p n j -> p (n j)"), w2_codes[:], w2_scales[:])
-        second_product(z_first, 0, HALF, "bank00", nc.vector.tensor_copy)
+        second_product(z_first, 0, HALF, "bank00", nc.scalar.copy)
         second_product(z_third, HALF, HALF // 2, "bank10", nc.scalar.copy)
-        second_product(z_fourth, HALF + HALF // 2, HALF // 2, "bank20", nc.scalar.copy)
+        second_product(z_fourth, HALF + HALF // 2, HALF // 2, "bank20", nc.vector.tensor_copy)

from contextlib import ExitStack

import concourse.mybir as mybir

K, T, S, H, N = 1024, 1024, 512, 512, 128
FLOPS = 2 * K * H * S + 2 * H * N * S

F32 = mybir.dt.float32
BF16 = mybir.dt.bfloat16
U32 = mybir.dt.uint32
U16 = mybir.dt.uint16
U8 = mybir.dt.uint8
FP8X4 = mybir.dt.float8_e4m3fn_x4
ACT = mybir.ActivationFunctionType
ALU = mybir.AluOpType

P = 128
PACK = 4
K_PASS = P * PACK
HALF = S // 2
LEAD = 4
SCALAR_COLS = 42
QUARTER = S // 4


def tile_picked_dconv_silu_e_kernel(tc, xT, w1, w2, taps, offs, out):
    nc = tc.nc

    with ExitStack() as ctx:
        keep = ctx.enter_context(tc.tile_pool(name="keep", bufs=1))
        psum = ctx.enter_context(tc.psum_pool(name="psum", bufs=1))

        def sbuf(shape, dtype, name):
            return keep.tile(shape, dtype, name=name, align_bytes=64)

        x_rows = xT.rearrange("(g p j) w -> g j p w", p=P, j=PACK)
        w1_rows = w1.rearrange("(g p j) c -> g p (j c)", p=P, j=PACK)
        x_raw, w1_raw = {}, {}

        def load_x(g, j):
            x_raw[g, j] = sbuf([P, T], F32, f"x_raw{g}{j}")
            nc.sync.dma_start(x_raw[g, j][:], x_rows[g, j])

        def load_w1(g):
            w1_raw[g] = sbuf([P, PACK * H], F32, f"w1_raw{g}")
            nc.sync.dma_start(w1_raw[g][:], w1_rows[g])

        load_x(0, 0)
        offsets = keep.tile([P, S // 16], U16, name="offsets")
        nc.sync.dma_start(offsets[:], offs)
        for j in range(1, PACK):
            load_x(0, j)
        load_x(1, 0)
        load_x(1, 1)
        load_w1(0)
        load_x(1, 2)
        load_x(1, 3)
        load_w1(1)
        tap = sbuf([P, PACK * 2], F32, "tap")
        nc.sync.dma_start(tap[:], taps.rearrange("(p t) d -> p (t d)", t=PACK))
        w2_raw = sbuf([P, PACK * N], F32, "w2_raw")
        nc.sync.dma_start(w2_raw[:], w2.rearrange("(p j) n -> p (j n)", j=PACK))

        delayed = sbuf([P, PACK, LEAD + S], F32, "delayed")
        zeros = sbuf([P, PACK], F32, "zeros")
        nc.gpsimd.memset(zeros[:], 0.0)
        nc.scalar.activation(delayed[:, :, LEAD - 1], zeros[:], ACT.Silu)

        def quantize(grouped_ap, codes, scales):
            nc.vector.quantize_mx(out=codes.bitcast(FP8X4), scales=scales, in_=grouped_ap)

        def shared(shape, dtype, name, tag):
            return keep.tile(shape, dtype, name=name, tag=tag, align_bytes=64)

        w1_grouped = [sbuf([P, PACK, P, PACK], BF16, "w1_grouped0")]
        w1_codes = [sbuf([P, H], U32, f"w1_codes{g}") for g in range(2)]
        w1_scales = [sbuf([P, H], U8, f"w1_scales{g}") for g in range(2)]
        x_codes, x_scales = {}, {}

        def entries(n0, n1):
            return offsets[:, n0 // 16 : n1 // 16]

        def gather(dst, g, j, n0=0, n1=S):
            nc.vector.tensor_copy(out=dst, in_=x_raw[g, j][:].indirect(entries(n0, n1)))

        def round_on_scalar(g, j):
            rounded = sbuf([P, T], BF16, f"rounded{g}")
            nc.scalar.activation(rounded[:], x_raw[g, j][:], ACT.Copy)
            return rounded

        def gather_on_scalar(dst, rounded, n0=0, n1=S):
            nc.scalar.activation(dst, rounded[:].indirect(entries(n0, n1)), ACT.Copy)

        def cast_w1(copy, g, m0, m1):
            copy(
                out=w1_grouped[g][:].rearrange("p t m j -> p m j t")[:, m0:m1],
                in_=w1_raw[g][:].rearrange("p (j m t) -> p m j t", j=PACK, t=PACK)[:, m0:m1],
            )

        def quantize_w1(g, t0, t1):
            cols = slice(t0 * P, t1 * P)
            quantize(w1_grouped[g][:, t0:t1].rearrange("p t m j -> p (t m j)"), w1_codes[g][:, cols], w1_scales[g][:, cols])

        picked_first = sbuf([P, PACK, S], BF16, "picked_first")
        gather(picked_first[:, 0, :], 0, 0)
        gather_on_scalar(picked_first[:, 1, :], round_on_scalar(0, 1))
        gather(picked_first[:, 2, :], 0, 2)
        gather(picked_first[:, 3, :], 0, 3)
        x_grouped_first = sbuf([P, S, PACK], BF16, "x_grouped_first")
        nc.scalar.copy(
            out=x_grouped_first[:].rearrange("p (c i) j -> p c j i", i=4),
            in_=picked_first[:].rearrange("p j (c i) -> p c j i", i=4),
        )
        pairs = [sbuf([P, 2, HALF], BF16, f"pair{u}") for u in range(2)]
        picked_late = sbuf([P, PACK, HALF], BF16, "picked_late")
        x_grouped = sbuf([P, HALF, PACK], BF16, "x_grouped")

        def weave_pair(copy, u):
            copy(out=x_grouped[:, :, 2 * u : 2 * u + 2], in_=pairs[u][:].rearrange("p e n -> p n e"))

        def gather_halves(j):
            gather(pairs[j // 2][:, j % 2, :], 1, j, 0, HALF)
            gather(picked_late[:, j, :], 1, j, HALF, S)

        gather_halves(0)
        gather_halves(1)
        codes_first = sbuf([P, S], U32, "codes_first")
        scales_first = sbuf([P, S], U8, "scales_first")
        quantize(x_grouped_first[:].rearrange("p n j -> p (n j)"), codes_first[:], scales_first[:])
        for h in range(2):
            x_codes[0, h] = codes_first[:, h * HALF : (h + 1) * HALF]
            x_scales[0, h] = scales_first[:, h * HALF : (h + 1) * HALF]
            x_codes[1, h] = sbuf([P, HALF], U32, f"x_codes{h}")[:]
        x_scales[1, 0] = sbuf([P, HALF], U8, "x_scales0")[:]
        weave_pair(nc.scalar.copy, 0)
        cast_w1(nc.vector.tensor_copy, 0, SCALAR_COLS, P)
        cast_w1(nc.scalar.copy, 0, 0, SCALAR_COLS)
        quantize_w1(0, 0, PACK)
        rounded = round_on_scalar(1, 2)
        gather_on_scalar(pairs[1][:, 0, :], rounded, 0, HALF)
        gather_on_scalar(picked_late[:, 2, :], rounded, HALF, S)
        gather_halves(3)
        weave_pair(nc.vector.tensor_copy, 1)
        quantize(x_grouped[:].rearrange("p n j -> p (n j)"), x_codes[1, 0], x_scales[1, 0])

        x_grouped_late = sbuf([P, HALF, PACK], BF16, "x_grouped_late")
        nc.scalar.copy(
            out=x_grouped_late[:].rearrange("p (c i) j -> p c j i", i=4),
            in_=picked_late[:].rearrange("p j (c i) -> p c j i", i=4),
        )

        banks = {}
        for h in range(2):
            for t in range(PACK):
                banks[t, h] = psum.tile([P, HALF], F32, name=f"h{t}{h}", tag=f"bank{t}{h}")

        def first_product(g, t, h):
            m_cols = slice(t * P, (t + 1) * P)
            nc.tensor.matmul_mx(
                out=banks[t, h][:],
                lhsT=w1_codes[g][:, m_cols].bitcast(FP8X4),
                lhsT_scale=w1_scales[g][:, m_cols],
                rhs=x_codes[g, h].bitcast(FP8X4),
                rhs_scale=x_scales[g, h],
                start=(g == 0),
                stop=(g == 1),
            )

        for h in range(2):
            for t in range(PACK):
                first_product(0, t, h)

        w1_late = [sbuf([P, 2, P, PACK], BF16, f"w1_late{u}") for u in range(2)]

        def cast_w1_late(copy, u, m0, m1):
            copy(
                out=w1_late[u][:].rearrange("p t m j -> p m j t")[:, m0:m1],
                in_=w1_raw[1][:].rearrange("p (j m t) -> p m j t", j=PACK, t=PACK)[:, m0:m1, :, 2 * u : 2 * u + 2],
            )

        cast_w1_late(nc.vector.tensor_copy, 0, 0, P)
        cast_w1_late(nc.vector.tensor_copy, 1, 0, P // 2)
        cast_w1_late(nc.scalar.copy, 1, P // 2, P)
        for t in range(PACK):
            cols = slice(t * P, (t + 1) * P)
            quantize(w1_late[t // 2][:, t % 2].rearrange("p m j -> p (m j)"), w1_codes[1][:, cols], w1_scales[1][:, cols])
        x_scales[1, 1] = shared([P, HALF], U8, "x_scales1", "w1_late0")[:]
        quantize(x_grouped_late[:].rearrange("p n j -> p (n j)"), x_codes[1, 1], x_scales[1, 1])
        for h in range(2):
            for t in range(PACK):
                first_product(1, t, h)

        w2_grouped = shared([P, N, PACK], BF16, "w2_grouped", "w1_late1")
        w2_codes = sbuf([P, N], U32, "w2_codes")
        w2_scales = sbuf([P, N], U8, "w2_scales")

        conv = {(1, c0): sbuf([P, PACK, QUARTER], F32, f"conv1{c0}") for c0 in (0, QUARTER)}
        conv[0, 0] = sbuf([P, PACK, HALF], F32, "conv00")

        def delay(t, h, on_vector):
            dst = delayed[:, t, LEAD + h * HALF : LEAD + (h + 1) * HALF]
            if on_vector:
                nc.vector.tensor_scalar(dst, banks[t, h][:], tap[:, 2 * t + 1 : 2 * t + 2], None, ALU.mult)
            else:
                nc.scalar.activation(dst, banks[t, h][:], ACT.Copy, scale=tap[:, 2 * t + 1 : 2 * t + 2])

        def convolve(t, h, c0=0, c1=HALF):
            nc.vector.scalar_tensor_tensor(
                out=conv[h, c0][:, t, :],
                in0=banks[t, h][:, c0:c1],
                scalar=tap[:, 2 * t : 2 * t + 1],
                in1=delayed[:, t, LEAD - 1 + h * HALF + c0 : LEAD - 1 + h * HALF + c1],
                op0=ALU.mult,
                op1=ALU.add,
            )

        def activate(h, c0, c1):
            z = sbuf([P, c1 - c0, PACK], BF16, f"z{h}{c0}")
            nc.scalar.activation(
                z[:].rearrange("p (c i) t -> p c t i", i=4),
                conv[h, c0][:].rearrange("p t (c i) -> p c t i", i=4),
                ACT.Silu,
            )
            return z

        def second_product(z, n0, width, tag, copy):
            z_codes = sbuf([P, width], U32, f"z_codes{n0}")
            z_scales = sbuf([P, width], U8, f"z_scales{n0}")
            quantize(z[:].rearrange("p n t -> p (n t)"), z_codes[:], z_scales[:])
            acc = psum.tile([P, width], F32, name=f"acc{n0}", tag=tag)
            nc.tensor.matmul_mx(
                out=acc[:],
                lhsT=w2_codes[:].bitcast(FP8X4),
                lhsT_scale=w2_scales[:],
                rhs=z_codes[:].bitcast(FP8X4),
                rhs_scale=z_scales[:],
                start=True,
                stop=True,
            )
            result = sbuf([P, width], F32, f"result{n0}")
            copy(out=result[:], in_=acc[:])
            nc.sync.dma_start(out[:, n0 : n0 + width], result[:])

        for t in range(PACK):
            delay(t, 0, t == 1)
        for t in range(PACK):
            convolve(t, 0)
        for t in range(PACK):
            delay(t, 1, t == 0)
        z_first = activate(0, 0, HALF)
        nc.gpsimd.tensor_copy(
            out=w2_grouped[:].rearrange("p n j -> p n j"),
            in_=w2_raw[:].rearrange("p (j n) -> p n j", j=PACK),
        )
        for t in range(PACK):
            convolve(t, 1, 0, HALF // 2)
        z_third = activate(1, 0, HALF // 2)
        for t in range(PACK):
            convolve(t, 1, HALF // 2, HALF)
        z_fourth = activate(1, HALF // 2, HALF)
        quantize(w2_grouped[:].rearrange("p n j -> p (n j)"), w2_codes[:], w2_scales[:])
        second_product(z_first, 0, HALF, "bank00", nc.scalar.copy)
        second_product(z_third, HALF, HALF // 2, "bank10", nc.scalar.copy)
        second_product(z_fourth, HALF + HALF // 2, HALF // 2, "bank20", nc.vector.tensor_copy)
